import numpy as np
import ml_dtypes


def mxq(x, axis, fmt="e4m3"):
    dtype, down = {"e4m3": (ml_dtypes.float8_e4m3fn, 7), "e5m2": (ml_dtypes.float8_e5m2, 14)}[fmt]
    v = np.moveaxis(np.asarray(x, np.float32).astype(ml_dtypes.bfloat16).astype(np.float64), axis, -1)
    blocks = v.reshape(v.shape[:-1] + (-1, 32))
    amax = np.abs(blocks).max(-1, keepdims=True)
    byte = np.maximum(np.where(amax > 0, np.frexp(amax)[1] - 1 + 127, 0) - down, 1)
    scale = np.exp2(byte - 127.0)
    codes = (blocks / scale).astype(np.float32).astype(dtype).astype(np.float64)
    return np.moveaxis((codes * scale).reshape(v.shape), -1, axis)


WIDE = False


def mx_kscale(k):
    if not WIDE:
        return np.ones(k)
    levels = np.array([10, -10, 5, -5, 0])
    if k % 512:
        return np.exp2(np.random.permutation(np.resize(levels, k // 32))).repeat(32)
    a = np.empty((k // 512, 16))
    for p in range(k // 512):
        a[p, :8] = np.random.permutation(np.resize(levels, 8))
        for g in range(8):
            far = levels[np.abs(levels - a[p, g]) >= 10]
            a[p, g + 8] = far[np.random.randint(len(far))]
    return np.exp2(a.ravel()).repeat(32)


BF16 = ml_dtypes.bfloat16


def bf(x):
    return np.asarray(x, np.float32).astype(BF16)


def f64(x):
    return np.asarray(x).astype(np.float64)

E4M3FN = np.array([(-1.0 if i & 128 else 1.0) * ((1.0 + (i & 7) / 8.0) * 2.0 ** (((i >> 3) & 15) - 7) if i & 120 else (i & 7) * 2.0 ** -9) for i in range(256)])


def e4m3fn_bytes(y):
    return np.clip(np.asarray(y, np.float64), -448.0, 448.0).astype(np.float32).astype(ml_dtypes.float8_e4m3fn).view(np.uint8)


def e4m3fn_values(b):
    return E4M3FN[b]


B, P, Q, C, N, G = 8, 16, 4, 128, 512, 128
T, K = B * P * P, Q * Q * C
SLOPE = 0.2
FMAX = 448.0


def setup_inputs():
    s = mx_kscale(K)
    image = np.random.standard_normal((B, P, Q, P, Q, C))
    x = image.transpose(0, 1, 3, 2, 4, 5).reshape(T, K) * s
    w = np.random.standard_normal((N, K)) / np.sqrt(K) / s
    x_scale = (np.abs(x).reshape(T, K // G, G).max(axis=2) / FMAX).astype(np.float32)
    w_scale = (np.abs(w).reshape(N // G, G, K // G, G).max(axis=(1, 3)) / FMAX).astype(np.float32)
    return {"x_bytes": e4m3fn_bytes(x / np.repeat(f64(x_scale), G, axis=1)),
            "x_scale": x_scale,
            "w_bytes": e4m3fn_bytes(w / np.repeat(np.repeat(f64(w_scale), G, axis=0), G, axis=1)),
            "w_scale": w_scale,
            "b": bf(0.4 * np.random.standard_normal(N))}


def reference(x_bytes, x_scale, w_bytes, w_scale, b):
    x = e4m3fn_values(x_bytes) * np.repeat(f64(x_scale), G, axis=1)
    w = e4m3fn_values(w_bytes) * np.repeat(np.repeat(f64(w_scale), G, axis=0), G, axis=1)
    z = (mxq(x, 1, "e4m3") @ mxq(w, 1, "e4m3").T) + f64(b)
    y = np.maximum(z, SLOPE * z)
    return y.reshape(B, P, P, N).transpose(0, 3, 1, 2)

@@ -1,0 +1,191 @@
+from contextlib import ExitStack
+
+import concourse.mybir as mybir
+from concourse.masks import make_identity
+
+F32 = mybir.dt.float32
+BF16 = mybir.dt.bfloat16
+U32 = mybir.dt.uint32
+U8 = mybir.dt.uint8
+FP8 = mybir.dt.float8_e4m3fn
+FP8X4 = mybir.dt.float8_e4m3fn_x4
+MULT = mybir.AluOpType.mult
+ADD = mybir.AluOpType.add
+MAX = mybir.AluOpType.max
+ACT = mybir.ActivationFunctionType
+
+T, K, N = 2048, 2048, 512
+FLOPS = 2 * T * K * N
+P = 128
+PASSES = 4
+KP = 512
+SLOPE = 0.2
+
+
+def tile_patch_convolution_leaky_relu_d2_kernel(tc, x_bytes, x_scale, w_bytes, w_scale, b, out):
+    nc = tc.nc
+    out_v = out.rearrange("i (p a) h v -> a p i (h v)", a=4)
+    with ExitStack() as ctx:
+        keep = ctx.enter_context(tc.tile_pool(name="keep", bufs=1))
+        byts = ctx.enter_context(tc.tile_pool(name="byts", bufs=8))
+        bigb = ctx.enter_context(tc.tile_pool(name="bigb", bufs=3))
+        wid = ctx.enter_context(tc.tile_pool(name="wid", bufs=4))
+        grp = ctx.enter_context(tc.tile_pool(name="grp", bufs=3))
+        wcp = ctx.enter_context(tc.tile_pool(name="wcp", bufs=4))
+        xcp = ctx.enter_context(tc.tile_pool(name="xcp", bufs=12))
+        ypool = ctx.enter_context(tc.tile_pool(name="ypool", bufs=4))
+        tps = ctx.enter_context(tc.psum_pool(name="tps", bufs=4))
+        aps = ctx.enter_context(tc.psum_pool(name="aps", bufs=4))
+
+        ws = keep.tile([P, 16], F32, name="ws")
+        for a in range(4):
+            nc.scalar.dma_start(out=ws[32 * a : 32 * a + 32, :], in_=w_scale[a].partition_broadcast(32))
+        xs_v = x_scale.rearrange("(m p) j -> p m j", p=P)
+        xs0 = keep.tile([P, 4, 16], F32, name="xs0")
+        nc.scalar.dma_start(out=xs0[:], in_=xs_v[:, 0:4, :])
+        bb = keep.tile([P, 4], BF16, name="bb")
+        nc.scalar.dma_start(out=bb[:], in_=b.rearrange("(p a) -> p a", a=4))
+        xs1 = keep.tile([P, 12, 16], F32, name="xs1")
+        nc.scalar.dma_start(out=xs1[:], in_=xs_v[:, 4:16, :])
+
+        w_v = w_bytes.rearrange("(p a) k -> p a k", a=4)
+        x_v = x_bytes.rearrange("(m p) k -> p m k", p=P)
+        wb, xb0, xb = {}, {}, {}
+        for g in (0, 3, 1, 2):
+            t = byts.tile([P, 4, KP], U8, name="byt")
+            nc.sync.dma_start(out=t[:], in_=w_v[:, :, KP * g : KP * g + KP])
+            wb[g] = t
+        for g in (0, 3, 1, 2):
+            t = byts.tile([P, 4, KP], U8, name="byt")
+            nc.sync.dma_start(out=t[:], in_=x_v[:, 0:4, KP * g : KP * g + KP])
+            xb0[g] = t
+        for M in range(1, 4):
+            t = bigb.tile([P, 4, K], U8, name="big")
+            nc.sync.dma_start(out=t[:], in_=x_v[:, 4 * M : 4 * M + 4, :])
+            xb[M] = t
+
+        ident = keep.tile([P, P], F32, name="ident")
+        make_identity(nc, ident[:])
+        b32 = keep.tile([P, 4], F32, name="b32")
+        nc.gpsimd.tensor_copy(out=b32[:], in_=bb[:])
+        b02 = keep.tile([P, 4], F32, name="b02")
+        nc.gpsimd.tensor_scalar(out=b02[:], in0=bb[:], scalar1=SLOPE, scalar2=None, op0=MULT)
+
+        def src(j, g, m, q):
+            if j == 0:
+                return wb[g][:, m, 128 * q : 128 * q + 128]
+            if j == 1:
+                return xb0[g][:, m, 128 * q : 128 * q + 128]
+            c = KP * g + 128 * q
+            return xb[j - 1][:, m, c : c + 128]
+
+        def scl(j, g, m, q):
+            c = 4 * g + q
+            if j == 0:
+                return ws[:, c : c + 1]
+            if j == 1:
+                return xs0[:, m, c : c + 1]
+            return xs1[:, 4 * (j - 2) + m, c : c + 1]
+
+        wide, grouped, codes, scales = {}, {}, {}, {}
+
+        def widen_v(j, i):
+            for blk in range(12 * i, 12 * i + 12):
+                g, m, q = blk // 16, (blk // 4) % 4, blk % 4
+                if (j, g) not in wide:
+                    wv = wid.tile([P, 4, 2, 256], BF16, name="wv", align_bytes=64)
+                    wide[j, g] = wv
+                o = wide[j, g][:, m, :, 64 * q : 64 * q + 64].rearrange("p u (b e) -> p b u e", e=16)
+                s = src(j, g, m, q).bitcast(FP8).rearrange("p (b u e) -> p b u e", b=4, u=2)
+                nc.vector.tensor_scalar(out=o, in0=s, scalar1=scl(j, g, m, q), scalar2=None, op0=MULT)
+
+        def widen_s(j, m):
+            if (j, 3) not in wide:
+                wsc = wid.tile([P, 4, KP], BF16, name="wsc", align_bytes=64)
+                wide[j, 3] = wsc
+            for q in range(4):
+                nc.scalar.activation(
+                    out=wide[j, 3][:, m, 128 * q : 128 * q + 128],
+                    in_=src(j, 3, m, q).bitcast(FP8),
+                    func=ACT.Copy,
+                    scale=scl(j, 3, m, q),
+                )
+
+        def turn(j, g):
+            gt = grp.tile([P, 4, P, 4], BF16, name="gt", align_bytes=64)
+            grouped[j, g] = gt
+            for h in range(2):
+                xt = tps.tile([P, 2, 2, P], F32, name="xt")
+                for mm in range(2):
+                    m = 2 * h + mm
+                    for u in range(2):
+                        if g < 3:
+                            w_in = wide[j, g][:, m, u, :].bitcast(F32)
+                        else:
+                            w_in = wide[j, g][:, m, :].bitcast(F32)[:, u : 256 : 2]
+                        nc.tensor.transpose(xt[:, mm, u, :], w_in, ident[:])
+                nc.scalar.copy(
+                    out=gt[:, 2 * h : 2 * h + 2, :, :].bitcast(F32),
+                    in_=xt[:].rearrange("p m u r -> p m r u"),
+                )
+
+        def quant(j, g):
+            pool = wcp if j == 0 else xcp
+            cd = pool.tile([P, 512], U32, name="cd", align_bytes=64)
+            sc = pool.tile([P, 512], U8, name="sc", align_bytes=64)
+            codes[j, g], scales[j, g] = cd, sc
+            nc.vector.quantize_mx(
+                out=cd[:].bitcast(FP8X4), scales=sc[:], in_=grouped[j, g][:].rearrange("p m r t -> p (m r t)")
+            )
+
+        accs = {}
+
+        def mm(j, n, g):
+            if g == 0:
+                acc = aps.tile([P, 512], F32, name="acc")
+                accs[j, n] = acc
+            nc.tensor.matmul_mx(
+                out=accs[j, n][:],
+                lhsT=codes[0, g][:, 128 * n : 128 * n + 128].bitcast(FP8X4),
+                lhsT_scale=scales[0, g][:, 128 * n : 128 * n + 128],
+                rhs=codes[j, g][:].bitcast(FP8X4),
+                rhs_scale=scales[j, g][:],
+                start=(g == 0),
+                stop=(g == 3),
+            )
+
+        def epi(j, n):
+            acc = accs[j, n]
+            low = ypool.tile([P, 512], F32, name="low")
+            nc.scalar.activation(out=low[:], in_=acc[:], func=ACT.Identity, bias=b02[:, n : n + 1], scale=SLOPE)
+            y = ypool.tile([P, 2, 256], F32, name="y")
+            nc.vector.scalar_tensor_tensor(
+                out=y[:].rearrange("p i t -> p (i t)"), in0=acc[:], scalar=b32[:, n : n + 1], in1=low[:], op0=ADD, op1=MAX
+            )
+            M = j - 1
+            nc.sync.dma_start(out=out_v[n, :, 2 * M : 2 * M + 2, :], in_=y[:])
+
+        mms = {}
+        for j in range(1, 4):
+            for n in range(4):
+                mms[4 * j + 7 + n] = [(j, n, g) for g in range(4)]
+        mms[21] = mms[21] + [(4, 0, 0), (4, 0, 1)]
+        mms[22] = mms[22] + [(4, 0, 2), (4, 1, 0), (4, 1, 1), (4, 1, 2)]
+        mms[23] = [(4, n, g) for n in (2, 3) for g in range(3)]
+        mms[23] = mms[23] + [(4, n, 3) for n in range(4)]
+
+        for s in range(28):
+            j, i = divmod(s, 4)
+            if s < 20:
+                widen_v(j, i)
+                widen_s(j, i)
+            if 2 <= s < 22:
+                turn((s - 2) // 4, (s - 2) % 4)
+            for e in mms.get(s, []):
+                mm(*e)
+            if 12 <= s < 24:
+                epi((s - 8) // 4, (s - 8) % 4)
+            if s >= 24:
+                epi(4, s - 24)
+            if 3 <= s < 23:
+                quant((s - 3) // 4, (s - 3) % 4)

@@ -27,42 +27,50 @@ def tile_patch_convolution_leaky_relu_d2_kernel(tc, x_bytes, x_scale, w_bytes, w
     out_v = out.rearrange("i (p a) h v -> a p i (h v)", a=4)
     with ExitStack() as ctx:
         keep = ctx.enter_context(tc.tile_pool(name="keep", bufs=1))
-        byts = ctx.enter_context(tc.tile_pool(name="byts", bufs=8))
+        byts = ctx.enter_context(tc.tile_pool(name="byts", bufs=6))
         bigb = ctx.enter_context(tc.tile_pool(name="bigb", bufs=3))
         wid = ctx.enter_context(tc.tile_pool(name="wid", bufs=4))
         grp = ctx.enter_context(tc.tile_pool(name="grp", bufs=3))
         wcp = ctx.enter_context(tc.tile_pool(name="wcp", bufs=4))
-        xcp = ctx.enter_context(tc.tile_pool(name="xcp", bufs=12))
+        xcp = ctx.enter_context(tc.tile_pool(name="xcp", bufs=16))
         ypool = ctx.enter_context(tc.tile_pool(name="ypool", bufs=4))
         tps = ctx.enter_context(tc.psum_pool(name="tps", bufs=4))
         aps = ctx.enter_context(tc.psum_pool(name="aps", bufs=4))
 
-        ws = keep.tile([P, 16], F32, name="ws")
-        for a in range(4):
-            nc.scalar.dma_start(out=ws[32 * a : 32 * a + 32, :], in_=w_scale[a].partition_broadcast(32))
         xs_v = x_scale.rearrange("(m p) j -> p m j", p=P)
         xs0 = keep.tile([P, 4, 16], F32, name="xs0")
         nc.scalar.dma_start(out=xs0[:], in_=xs_v[:, 0:4, :])
+        ws = keep.tile([P, 16], F32, name="ws")
+        for a in range(4):
+            nc.scalar.dma_start(out=ws[32 * a : 32 * a + 32, :], in_=w_scale[a].partition_broadcast(32))
         bb = keep.tile([P, 4], BF16, name="bb")
         nc.scalar.dma_start(out=bb[:], in_=b.rearrange("(p a) -> p a", a=4))
         xs1 = keep.tile([P, 12, 16], F32, name="xs1")
-        nc.scalar.dma_start(out=xs1[:], in_=xs_v[:, 4:16, :])
 
         w_v = w_bytes.rearrange("(p a) k -> p a k", a=4)
         x_v = x_bytes.rearrange("(m p) k -> p m k", p=P)
-        wb, xb0, xb = {}, {}, {}
-        for g in (0, 3, 1, 2):
-            t = byts.tile([P, 4, KP], U8, name="byt")
-            nc.sync.dma_start(out=t[:], in_=w_v[:, :, KP * g : KP * g + KP])
-            wb[g] = t
-        for g in (0, 3, 1, 2):
-            t = byts.tile([P, 4, KP], U8, name="byt")
-            nc.sync.dma_start(out=t[:], in_=x_v[:, 0:4, KP * g : KP * g + KP])
-            xb0[g] = t
+        xb = {}
+        for h, g in ((0, 0), (0, 3), (1, 0), (1, 3)):
+            t = byts.tile([P, 2, KP], U8, name="bhalf")
+            nc.sync.dma_start(out=t[:], in_=x_v[:, 2 * h : 2 * h + 2, KP * g : KP * g + KP])
+            xb[0, 2 * h, g] = (t, 0, 0)
+            xb[0, 2 * h + 1, g] = (t, 1, 0)
+        for v, j, gs in ((x_v, 0, (1, 2)), (w_v, 1, (0, 3, 1, 2))):
+            for g in gs:
+                t = byts.tile([P, 4, KP], U8, name="byt")
+                nc.sync.dma_start(out=t[:], in_=v[:, 0:4, KP * g : KP * g + KP])
+                for m in range(4):
+                    xb[j, m, g] = (t, m, 0)
+        nc.sync.dma_start(out=xs1[:], in_=xs_v[:, 4:16, :])
         for M in range(1, 4):
             t = bigb.tile([P, 4, K], U8, name="big")
             nc.sync.dma_start(out=t[:], in_=x_v[:, 4 * M : 4 * M + 4, :])
-            xb[M] = t
+            for m in range(4):
+                for g in range(4):
+                    if M < 3:
+                        xb[M + 1, m, g] = (t, m, KP * g)
+                    else:
+                        xb[4 + m // 2, m % 2, g] = (t, m, KP * g)
 
         ident = keep.tile([P, P], F32, name="ident")
         make_identity(nc, ident[:])
@@ -71,27 +79,27 @@ def tile_patch_convolution_leaky_relu_d2_kernel(tc, x_bytes, x_scale, w_bytes, w
         b02 = keep.tile([P, 4], F32, name="b02")
         nc.gpsimd.tensor_scalar(out=b02[:], in0=bb[:], scalar1=SLOPE, scalar2=None, op0=MULT)
 
+        NT = [4, 4, 4, 4, 2, 2]
+        FIRST = [0, 0, 4, 8, 12, 14]
+
         def src(j, g, m, q):
-            if j == 0:
-                return wb[g][:, m, 128 * q : 128 * q + 128]
-            if j == 1:
-                return xb0[g][:, m, 128 * q : 128 * q + 128]
-            c = KP * g + 128 * q
-            return xb[j - 1][:, m, c : c + 128]
+            t, mi, c = xb[j, m, g]
+            return t[:, mi, c + 128 * q : c + 128 * q + 128]
 
         def scl(j, g, m, q):
             c = 4 * g + q
-            if j == 0:
-                return ws[:, c : c + 1]
             if j == 1:
+                return ws[:, c : c + 1]
+            if j == 0:
                 return xs0[:, m, c : c + 1]
-            return xs1[:, 4 * (j - 2) + m, c : c + 1]
+            return xs1[:, FIRST[j] - 4 + m, c : c + 1]
 
         wide, grouped, codes, scales = {}, {}, {}, {}
 
         def widen_v(j, i):
-            for blk in range(12 * i, 12 * i + 12):
-                g, m, q = blk // 16, (blk // 4) % 4, blk % 4
+            n = 3 * NT[j]
+            for blk in range(n * i, n * i + n):
+                g, m, q = blk // (4 * NT[j]), (blk // 4) % NT[j], blk % 4
                 if (j, g) not in wide:
                     wv = wid.tile([P, 4, 2, 256], BF16, name="wv", align_bytes=64)
                     wide[j, g] = wv
@@ -99,22 +107,23 @@ def tile_patch_convolution_leaky_relu_d2_kernel(tc, x_bytes, x_scale, w_bytes, w
                 s = src(j, g, m, q).bitcast(FP8).rearrange("p (b u e) -> p b u e", b=4, u=2)
                 nc.vector.tensor_scalar(out=o, in0=s, scalar1=scl(j, g, m, q), scalar2=None, op0=MULT)
 
-        def widen_s(j, m):
+        def widen_3(j, i):
             if (j, 3) not in wide:
                 wsc = wid.tile([P, 4, KP], BF16, name="wsc", align_bytes=64)
                 wide[j, 3] = wsc
-            for q in range(4):
-                nc.scalar.activation(
-                    out=wide[j, 3][:, m, 128 * q : 128 * q + 128],
-                    in_=src(j, 3, m, q).bitcast(FP8),
-                    func=ACT.Copy,
-                    scale=scl(j, 3, m, q),
-                )
+            for blk in range(NT[j] * i, NT[j] * i + NT[j]):
+                m, q = blk // 4, blk % 4
+                o = wide[j, 3][:, m, 128 * q : 128 * q + 128]
+                s = src(j, 3, m, q).bitcast(FP8)
+                if j == 5:
+                    nc.vector.tensor_scalar(out=o, in0=s, scalar1=scl(j, 3, m, q), scalar2=None, op0=MULT)
+                else:
+                    nc.scalar.activation(out=o, in_=s, func=ACT.Copy, scale=scl(j, 3, m, q))
 
         def turn(j, g):
             gt = grp.tile([P, 4, P, 4], BF16, name="gt", align_bytes=64)
             grouped[j, g] = gt
-            for h in range(2):
+            for h in range(NT[j] // 2):
                 xt = tps.tile([P, 2, 2, P], F32, name="xt")
                 for mm in range(2):
                     m = 2 * h + mm
@@ -130,62 +139,85 @@ def tile_patch_convolution_leaky_relu_d2_kernel(tc, x_bytes, x_scale, w_bytes, w
                 )
 
         def quant(j, g):
-            pool = wcp if j == 0 else xcp
+            w = NT[j] * P
+            pool = wcp if j == 1 else xcp
             cd = pool.tile([P, 512], U32, name="cd", align_bytes=64)
             sc = pool.tile([P, 512], U8, name="sc", align_bytes=64)
             codes[j, g], scales[j, g] = cd, sc
             nc.vector.quantize_mx(
-                out=cd[:].bitcast(FP8X4), scales=sc[:], in_=grouped[j, g][:].rearrange("p m r t -> p (m r t)")
+                out=cd[:, 0:w].bitcast(FP8X4),
+                scales=sc[:, 0:w],
+                in_=grouped[j, g][:, 0 : NT[j], :, :].rearrange("p m r t -> p (m r t)"),
             )
 
-        accs = {}
+        accs, lows = {}, {}
 
         def mm(j, n, g):
+            w = NT[j] * P
             if g == 0:
                 acc = aps.tile([P, 512], F32, name="acc")
                 accs[j, n] = acc
             nc.tensor.matmul_mx(
-                out=accs[j, n][:],
-                lhsT=codes[0, g][:, 128 * n : 128 * n + 128].bitcast(FP8X4),
-                lhsT_scale=scales[0, g][:, 128 * n : 128 * n + 128],
-                rhs=codes[j, g][:].bitcast(FP8X4),
-                rhs_scale=scales[j, g][:],
+                out=accs[j, n][:, 0:w],
+                lhsT=codes[1, g][:, 128 * n : 128 * n + 128].bitcast(FP8X4),
+                lhsT_scale=scales[1, g][:, 128 * n : 128 * n + 128],
+                rhs=codes[j, g][:, 0:w].bitcast(FP8X4),
+                rhs_scale=scales[j, g][:, 0:w],
                 start=(g == 0),
                 stop=(g == 3),
             )
 
-        def epi(j, n):
-            acc = accs[j, n]
+        def epi_s(j, n):
+            w = NT[j] * P
             low = ypool.tile([P, 512], F32, name="low")
-            nc.scalar.activation(out=low[:], in_=acc[:], func=ACT.Identity, bias=b02[:, n : n + 1], scale=SLOPE)
-            y = ypool.tile([P, 2, 256], F32, name="y")
-            nc.vector.scalar_tensor_tensor(
-                out=y[:].rearrange("p i t -> p (i t)"), in0=acc[:], scalar=b32[:, n : n + 1], in1=low[:], op0=ADD, op1=MAX
+            lows[j, n] = low
+            nc.scalar.activation(
+                out=low[:, 0:w], in_=accs[j, n][:, 0:w], func=ACT.Identity, bias=b02[:, n : n + 1], scale=SLOPE
             )
-            M = j - 1
-            nc.sync.dma_start(out=out_v[n, :, 2 * M : 2 * M + 2, :], in_=y[:])
 
-        mms = {}
-        for j in range(1, 4):
+        def epi_v(j, n):
+            w = NT[j] * P
+            y = ypool.tile([P, 512], F32, name="y")
+            nc.vector.scalar_tensor_tensor(
+                out=y[:, 0:w], in0=accs[j, n][:, 0:w], scalar=b32[:, n : n + 1], in1=lows[j, n][:, 0:w], op0=ADD, op1=MAX
+            )
+            i0 = FIRST[j] // 2
+            nc.sync.dma_start(
+                out=out_v[n, :, i0 : i0 + NT[j] // 2, :], in_=y[:, 0:w].rearrange("p (i t) -> p i t", t=256)
+            )
+
+        mms, epis = {}, {}
+        for j, s0 in ((0, 11), (2, 15), (3, 19)):
             for n in range(4):
-                mms[4 * j + 7 + n] = [(j, n, g) for g in range(4)]
-        mms[21] = mms[21] + [(4, 0, 0), (4, 0, 1)]
-        mms[22] = mms[22] + [(4, 0, 2), (4, 1, 0), (4, 1, 1), (4, 1, 2)]
-        mms[23] = [(4, n, g) for n in (2, 3) for g in range(3)]
-        mms[23] = mms[23] + [(4, n, 3) for n in range(4)]
+                mms[s0 + n] = [(j, n, g) for g in range(4)]
+                epis[s0 + n + 1] = [(j, n)]
+        for h in range(2):
+            mms[23 + h] = [(4, n, g) for n in (2 * h, 2 * h + 1) for g in range(4)]
+            epis[24 + h] = [(4, 2 * h), (4, 2 * h + 1)]
+        mms[26] = [(5, n, g) for n in range(4) for g in range(3)]
+        mms[27] = [(5, n, 3) for n in range(4)]
 
+        pinned = ctx.enter_context(
+            tc.manual_schedule(
+                engines={mybir.EngineType.PE, mybir.EngineType.Activation, mybir.EngineType.DVE, mybir.EngineType.SP}
+            )
+        )
         for s in range(28):
             j, i = divmod(s, 4)
-            if s < 20:
-                widen_v(j, i)
-                widen_s(j, i)
-            if 2 <= s < 22:
+            for e in epis.get(s, []):
+                epi_s(*e)
+            if s < 24:
+                widen_3(j, i)
+            if 2 <= s < 26:
                 turn((s - 2) // 4, (s - 2) % 4)
-            for e in mms.get(s, []):
-                mm(*e)
-            if 12 <= s < 24:
-                epi((s - 8) // 4, (s - 8) % 4)
-            if s >= 24:
-                epi(4, s - 24)
-            if 3 <= s < 23:
+            for x in mms.get(s, []):
+                mm(*x)
+            if s < 24:
+                widen_v(j, i)
+            for e in epis.get(s, []):
+                epi_v(*e)
+            if 3 <= s < 27:
                 quant((s - 3) // 4, (s - 3) % 4)
+        for n in range(4):
+            epi_s(5, n)
+            epi_v(5, n)

@@ -29,7 +29,7 @@ def tile_patch_convolution_leaky_relu_d2_kernel(tc, x_bytes, x_scale, w_bytes, w
         keep = ctx.enter_context(tc.tile_pool(name="keep", bufs=1))
         byts = ctx.enter_context(tc.tile_pool(name="byts", bufs=6))
         bigb = ctx.enter_context(tc.tile_pool(name="bigb", bufs=3))
-        wid = ctx.enter_context(tc.tile_pool(name="wid", bufs=4))
+        wid = ctx.enter_context(tc.tile_pool(name="wid", bufs=8))
         grp = ctx.enter_context(tc.tile_pool(name="grp", bufs=3))
         wcp = ctx.enter_context(tc.tile_pool(name="wcp", bufs=4))
         xcp = ctx.enter_context(tc.tile_pool(name="xcp", bufs=16))
@@ -96,29 +96,41 @@ def tile_patch_convolution_leaky_relu_d2_kernel(tc, x_bytes, x_scale, w_bytes, w
 
         wide, grouped, codes, scales = {}, {}, {}, {}
 
+        def lists(j):
+            nt = NT[j]
+            s2 = S2[j]
+            v = [(g, m, q) for g in range(3) for m in range(nt) for q in range(4) if g < 2 or m < nt - s2]
+            s = [(2, m, q) for m in range(nt - s2, nt) for q in range(4)]
+            s = s + [(3, m, q) for m in range(nt) for q in range(4)]
+            return v, s
+
+        S2 = [1, 1, 1, 1, 0, 0]
+
         def widen_v(j, i):
-            n = 3 * NT[j]
-            for blk in range(n * i, n * i + n):
-                g, m, q = blk // (4 * NT[j]), (blk // 4) % NT[j], blk % 4
+            v = lists(j)[0]
+            n = len(v) // 4
+            for g, m, q in v[n * i : n * i + n]:
                 if (j, g) not in wide:
                     wv = wid.tile([P, 4, 2, 256], BF16, name="wv", align_bytes=64)
                     wide[j, g] = wv
-                o = wide[j, g][:, m, :, 64 * q : 64 * q + 64].rearrange("p u (b e) -> p b u e", e=16)
-                s = src(j, g, m, q).bitcast(FP8).rearrange("p (b u e) -> p b u e", b=4, u=2)
+                s = src(j, g, m, q).bitcast(FP8)
+                if g < 2:
+                    o = wide[j, g][:, m, :, 64 * q : 64 * q + 64].rearrange("p u (b e) -> p b u e", e=16)
+                    s = s.rearrange("p (b u e) -> p b u e", b=4, u=2)
+                else:
+                    o = wide[j, g][:, m, :, :].rearrange("p u e -> p (u e)")[:, 128 * q : 128 * q + 128]
                 nc.vector.tensor_scalar(out=o, in0=s, scalar1=scl(j, g, m, q), scalar2=None, op0=MULT)
 
         def widen_3(j, i):
-            if (j, 3) not in wide:
-                wsc = wid.tile([P, 4, KP], BF16, name="wsc", align_bytes=64)
-                wide[j, 3] = wsc
-            for blk in range(NT[j] * i, NT[j] * i + NT[j]):
-                m, q = blk // 4, blk % 4
-                o = wide[j, 3][:, m, 128 * q : 128 * q + 128]
-                s = src(j, 3, m, q).bitcast(FP8)
-                if j == 5:
-                    nc.vector.tensor_scalar(out=o, in0=s, scalar1=scl(j, 3, m, q), scalar2=None, op0=MULT)
-                else:
-                    nc.scalar.activation(out=o, in_=s, func=ACT.Copy, scale=scl(j, 3, m, q))
+            v = lists(j)[1]
+            n = len(v) // 4
+            for g, m, q in v[n * i : n * i + n]:
+                if (j, g) not in wide:
+                    wv = wid.tile([P, 4, 2, 256], BF16, name="wv", align_bytes=64)
+                    wide[j, g] = wv
+                o = wide[j, g][:, m, :, :].rearrange("p u e -> p (u e)")[:, 128 * q : 128 * q + 128]
+                s = src(j, g, m, q).bitcast(FP8)
+                nc.scalar.activation(out=o, in_=s, func=ACT.Copy, scale=scl(j, g, m, q))
 
         def turn(j, g):
             gt = grp.tile([P, 4, P, 4], BF16, name="gt", align_bytes=64)
@@ -128,10 +140,10 @@ def tile_patch_convolution_leaky_relu_d2_kernel(tc, x_bytes, x_scale, w_bytes, w
                 for mm in range(2):
                     m = 2 * h + mm
                     for u in range(2):
-                        if g < 3:
+                        if g < 2:
                             w_in = wide[j, g][:, m, u, :].bitcast(F32)
                         else:
-                            w_in = wide[j, g][:, m, :].bitcast(F32)[:, u : 256 : 2]
+                            w_in = wide[j, g][:, m, :, :].rearrange("p u e -> p (u e)").bitcast(F32)[:, u : 256 : 2]
                         nc.tensor.transpose(xt[:, mm, u, :], w_in, ident[:])
                 nc.scalar.copy(
                     out=gt[:, 2 * h : 2 * h + 2, :, :].bitcast(F32),

@@ -50,12 +50,21 @@ def tile_patch_convolution_leaky_relu_d2_kernel(tc, x_bytes, x_scale, w_bytes, w
         w_v = w_bytes.rearrange("(p a) k -> p a k", a=4)
         x_v = x_bytes.rearrange("(m p) k -> p m k", p=P)
         xb = {}
-        for h, g in ((0, 0), (0, 3), (1, 0), (1, 3)):
+        for h, g in ((0, 0), (1, 0), (1, 3)):
             t = byts.tile([P, 2, KP], U8, name="bhalf")
             nc.sync.dma_start(out=t[:], in_=x_v[:, 2 * h : 2 * h + 2, KP * g : KP * g + KP])
             xb[0, 2 * h, g] = (t, 0, 0)
             xb[0, 2 * h + 1, g] = (t, 1, 0)
-        for v, j, gs in ((x_v, 0, (1, 2)), (w_v, 1, (0, 3, 1, 2))):
+        for g in (1, 2):
+            t = byts.tile([P, 4, KP], U8, name="byt")
+            nc.sync.dma_start(out=t[:], in_=x_v[:, 0:4, KP * g : KP * g + KP])
+            for m in range(4):
+                xb[0, m, g] = (t, m, 0)
+        t = byts.tile([P, 2, KP], U8, name="bhalf")
+        nc.sync.dma_start(out=t[:], in_=x_v[:, 0:2, KP * 3 : KP * 3 + KP])
+        xb[0, 0, 3] = (t, 0, 0)
+        xb[0, 1, 3] = (t, 1, 0)
+        for v, j, gs in ((w_v, 1, (0, 3, 1, 2)),):
             for g in gs:
                 t = byts.tile([P, 4, KP], U8, name="byt")
                 nc.sync.dma_start(out=t[:], in_=v[:, 0:4, KP * g : KP * g + KP])
@@ -98,13 +107,11 @@ def tile_patch_convolution_leaky_relu_d2_kernel(tc, x_bytes, x_scale, w_bytes, w
 
         def lists(j):
             nt = NT[j]
-            s2 = S2[j]
-            v = [(g, m, q) for g in range(3) for m in range(nt) for q in range(4) if g < 2 or m < nt - s2]
-            s = [(2, m, q) for m in range(nt - s2, nt) for q in range(4)]
-            s = s + [(3, m, q) for m in range(nt) for q in range(4)]
+            v = [(g, m, q) for g in range(4) for m in range(nt) for q in range(4) if g < 3 or m < nt - S3[j]]
+            s = [(3, m, q) for m in range(nt - S3[j], nt) for q in range(4)]
             return v, s
 
-        S2 = [1, 1, 1, 1, 0, 0]
+        S3 = [2,2,2,2,1,0]
 
         def widen_v(j, i):
             v = lists(j)[0]
@@ -114,7 +121,7 @@ def tile_patch_convolution_leaky_relu_d2_kernel(tc, x_bytes, x_scale, w_bytes, w
                     wv = wid.tile([P, 4, 2, 256], BF16, name="wv", align_bytes=64)
                     wide[j, g] = wv
                 s = src(j, g, m, q).bitcast(FP8)
-                if g < 2:
+                if g < 3:
                     o = wide[j, g][:, m, :, 64 * q : 64 * q + 64].rearrange("p u (b e) -> p b u e", e=16)
                     s = s.rearrange("p (b u e) -> p b u e", b=4, u=2)
                 else:
@@ -140,7 +147,7 @@ def tile_patch_convolution_leaky_relu_d2_kernel(tc, x_bytes, x_scale, w_bytes, w
                 for mm in range(2):
                     m = 2 * h + mm
                     for u in range(2):
-                        if g < 2:
+                        if g < 3:
                             w_in = wide[j, g][:, m, u, :].bitcast(F32)
                         else:
                             w_in = wide[j, g][:, m, :, :].rearrange("p u e -> p (u e)").bitcast(F32)[:, u : 256 : 2]

@@ -31,9 +31,9 @@ def tile_patch_convolution_leaky_relu_d2_kernel(tc, x_bytes, x_scale, w_bytes, w
         bigb = ctx.enter_context(tc.tile_pool(name="bigb", bufs=3))
         wid = ctx.enter_context(tc.tile_pool(name="wid", bufs=8))
         grp = ctx.enter_context(tc.tile_pool(name="grp", bufs=3))
-        wcp = ctx.enter_context(tc.tile_pool(name="wcp", bufs=4))
-        xcp = ctx.enter_context(tc.tile_pool(name="xcp", bufs=16))
-        ypool = ctx.enter_context(tc.tile_pool(name="ypool", bufs=4))
+        wcp = ctx.enter_context(tc.tile_pool(name="wcp", bufs=2))
+        xcp = ctx.enter_context(tc.tile_pool(name="xcp", bufs=10))
+        ypool = ctx.enter_context(tc.tile_pool(name="ypool", bufs=8))
         tps = ctx.enter_context(tc.psum_pool(name="tps", bufs=4))
         aps = ctx.enter_context(tc.psum_pool(name="aps", bufs=4))
 
@@ -50,7 +50,7 @@ def tile_patch_convolution_leaky_relu_d2_kernel(tc, x_bytes, x_scale, w_bytes, w
         w_v = w_bytes.rearrange("(p a) k -> p a k", a=4)
         x_v = x_bytes.rearrange("(m p) k -> p m k", p=P)
         xb = {}
-        for h, g in ((0, 0), (1, 0), (1, 3)):
+        for h, g in ((0, 0), (1, 0), (1, 3), (0, 3)):
             t = byts.tile([P, 2, KP], U8, name="bhalf")
             nc.sync.dma_start(out=t[:], in_=x_v[:, 2 * h : 2 * h + 2, KP * g : KP * g + KP])
             xb[0, 2 * h, g] = (t, 0, 0)
@@ -60,10 +60,6 @@ def tile_patch_convolution_leaky_relu_d2_kernel(tc, x_bytes, x_scale, w_bytes, w
             nc.sync.dma_start(out=t[:], in_=x_v[:, 0:4, KP * g : KP * g + KP])
             for m in range(4):
                 xb[0, m, g] = (t, m, 0)
-        t = byts.tile([P, 2, KP], U8, name="bhalf")
-        nc.sync.dma_start(out=t[:], in_=x_v[:, 0:2, KP * 3 : KP * 3 + KP])
-        xb[0, 0, 3] = (t, 0, 0)
-        xb[0, 1, 3] = (t, 1, 0)
         for v, j, gs in ((w_v, 1, (0, 3, 1, 2)),):
             for g in gs:
                 t = byts.tile([P, 4, KP], U8, name="byt")
@@ -108,10 +104,10 @@ def tile_patch_convolution_leaky_relu_d2_kernel(tc, x_bytes, x_scale, w_bytes, w
         def lists(j):
             nt = NT[j]
             v = [(g, m, q) for g in range(4) for m in range(nt) for q in range(4) if g < 3 or m < nt - S3[j]]
-            s = [(3, m, q) for m in range(nt - S3[j], nt) for q in range(4)]
+            s = [(3, m, q) for m in reversed(range(nt - S3[j], nt)) for q in range(4)]
             return v, s
 
-        S3 = [2,2,2,2,1,0]
+        S3 = [3,3,3,3,1,1]
 
         def widen_v(j, i):
             v = lists(j)[0]
@@ -139,10 +135,20 @@ def tile_patch_convolution_leaky_relu_d2_kernel(tc, x_bytes, x_scale, w_bytes, w
                 s = src(j, g, m, q).bitcast(FP8)
                 nc.scalar.activation(out=o, in_=s, func=ACT.Copy, scale=scl(j, g, m, q))
 
+        def together(j, g):
+            if j == 5 and g >= 2:
+                return [g]
+            return [g - g % 2, g - g % 2 + 1]
+
         def turn(j, g):
-            gt = grp.tile([P, 4, P, 4], BF16, name="gt", align_bytes=64)
-            grouped[j, g] = gt
-            for h in range(NT[j] // 2):
+            nt = NT[j]
+            ps = together(j, g)
+            if g == ps[0]:
+                gt = grp.tile([P, 8, P, 4], BF16, name="gt", align_bytes=64)
+                for x in ps:
+                    grouped[j, x] = gt
+            c = nt * (g - ps[0])
+            for h in range(nt // 2):
                 xt = tps.tile([P, 2, 2, P], F32, name="xt")
                 for mm in range(2):
                     m = 2 * h + mm
@@ -153,20 +159,26 @@ def tile_patch_convolution_leaky_relu_d2_kernel(tc, x_bytes, x_scale, w_bytes, w
                             w_in = wide[j, g][:, m, :, :].rearrange("p u e -> p (u e)").bitcast(F32)[:, u : 256 : 2]
                         nc.tensor.transpose(xt[:, mm, u, :], w_in, ident[:])
                 nc.scalar.copy(
-                    out=gt[:, 2 * h : 2 * h + 2, :, :].bitcast(F32),
+                    out=grouped[j, g][:, c + 2 * h : c + 2 * h + 2, :, :].bitcast(F32),
                     in_=xt[:].rearrange("p m u r -> p m r u"),
                 )
 
         def quant(j, g):
-            w = NT[j] * P
+            ps = together(j, g)
+            if g != ps[-1]:
+                return
+            nt = NT[j]
+            w = nt * P * len(ps)
             pool = wcp if j == 1 else xcp
-            cd = pool.tile([P, 512], U32, name="cd", align_bytes=64)
-            sc = pool.tile([P, 512], U8, name="sc", align_bytes=64)
-            codes[j, g], scales[j, g] = cd, sc
+            cd = pool.tile([P, 1024], U32, name="cd", align_bytes=64)
+            sc = pool.tile([P, 1024], U8, name="sc", align_bytes=64)
+            for x in ps:
+                o = nt * P * (x - ps[0])
+                codes[j, x], scales[j, x] = cd[:, o : o + nt * P], sc[:, o : o + nt * P]
             nc.vector.quantize_mx(
                 out=cd[:, 0:w].bitcast(FP8X4),
                 scales=sc[:, 0:w],
-                in_=grouped[j, g][:, 0 : NT[j], :, :].rearrange("p m r t -> p (m r t)"),
+                in_=grouped[j, g][:, 0 : nt * len(ps), :, :].rearrange("p m r t -> p (m r t)"),
             )
 
         accs, lows = {}, {}
@@ -180,8 +192,8 @@ def tile_patch_convolution_leaky_relu_d2_kernel(tc, x_bytes, x_scale, w_bytes, w
                 out=accs[j, n][:, 0:w],
                 lhsT=codes[1, g][:, 128 * n : 128 * n + 128].bitcast(FP8X4),
                 lhsT_scale=scales[1, g][:, 128 * n : 128 * n + 128],
-                rhs=codes[j, g][:, 0:w].bitcast(FP8X4),
-                rhs_scale=scales[j, g][:, 0:w],
+                rhs=codes[j, g].bitcast(FP8X4),
+                rhs_scale=scales[j, g],
                 start=(g == 0),
                 stop=(g == 3),
             )
@@ -210,33 +222,50 @@ def tile_patch_convolution_leaky_relu_d2_kernel(tc, x_bytes, x_scale, w_bytes, w
             for n in range(4):
                 mms[s0 + n] = [(j, n, g) for g in range(4)]
                 epis[s0 + n + 1] = [(j, n)]
-        for h in range(2):
-            mms[23 + h] = [(4, n, g) for n in (2 * h, 2 * h + 1) for g in range(4)]
-            epis[24 + h] = [(4, 2 * h), (4, 2 * h + 1)]
-        mms[26] = [(5, n, g) for n in range(4) for g in range(3)]
-        mms[27] = [(5, n, 3) for n in range(4)]
+        mms[23] = [(4, n, g) for n in (0, 1) for g in range(4)]
 
         pinned = ctx.enter_context(
             tc.manual_schedule(
                 engines={mybir.EngineType.PE, mybir.EngineType.Activation, mybir.EngineType.DVE, mybir.EngineType.SP}
             )
         )
-        for s in range(28):
+        for s in range(24):
             j, i = divmod(s, 4)
+            widen_3(j, i)
             for e in epis.get(s, []):
                 epi_s(*e)
-            if s < 24:
-                widen_3(j, i)
-            if 2 <= s < 26:
+            if s >= 2:
                 turn((s - 2) // 4, (s - 2) % 4)
             for x in mms.get(s, []):
                 mm(*x)
-            if s < 24:
-                widen_v(j, i)
+            widen_v(j, i)
+            if s >= 3:
+                quant((s - 3) // 4, (s - 3) % 4)
             for e in epis.get(s, []):
                 epi_v(*e)
-            if 3 <= s < 27:
-                quant((s - 3) // 4, (s - 3) % 4)
+        epi_s(4, 0)
+        epi_v(4, 0)
+        quant(5, 1)
+        turn(5, 2)
+        turn(5, 3)
+        epi_s(4, 1)
+        for n in (2, 3):
+            for g in range(4):
+                mm(4, n, g)
+        quant(5, 2)
+        epi_v(4, 1)
+        for n in (0, 1):
+            for g in range(3):
+                mm(5, n, g)
+        quant(5, 3)
+        for n in (2, 3):
+            epi_s(4, n)
+            epi_v(4, n)
+        for n in (0, 1):
+            mm(5, n, 3)
+        for n in (2, 3):
+            for g in range(4):
+                mm(5, n, g)
         for n in range(4):
             epi_s(5, n)
             epi_v(5, n)

from contextlib import ExitStack

import concourse.mybir as mybir
from concourse.masks import make_identity

F32 = mybir.dt.float32
BF16 = mybir.dt.bfloat16
U32 = mybir.dt.uint32
U8 = mybir.dt.uint8
FP8 = mybir.dt.float8_e4m3fn
FP8X4 = mybir.dt.float8_e4m3fn_x4
MULT = mybir.AluOpType.mult
ADD = mybir.AluOpType.add
MAX = mybir.AluOpType.max
ACT = mybir.ActivationFunctionType

T, K, N = 2048, 2048, 512
FLOPS = 2 * T * K * N
P = 128
PASSES = 4
KP = 512
SLOPE = 0.2


def tile_patch_convolution_leaky_relu_d2_kernel(tc, x_bytes, x_scale, w_bytes, w_scale, b, out):
    nc = tc.nc
    out_v = out.rearrange("i (p a) h v -> a p i (h v)", a=4)
    with ExitStack() as ctx:
        keep = ctx.enter_context(tc.tile_pool(name="keep", bufs=1))
        byts = ctx.enter_context(tc.tile_pool(name="byts", bufs=6))
        bigb = ctx.enter_context(tc.tile_pool(name="bigb", bufs=3))
        wid = ctx.enter_context(tc.tile_pool(name="wid", bufs=8))
        grp = ctx.enter_context(tc.tile_pool(name="grp", bufs=3))
        wcp = ctx.enter_context(tc.tile_pool(name="wcp", bufs=2))
        xcp = ctx.enter_context(tc.tile_pool(name="xcp", bufs=10))
        ypool = ctx.enter_context(tc.tile_pool(name="ypool", bufs=8))
        tps = ctx.enter_context(tc.psum_pool(name="tps", bufs=4))
        aps = ctx.enter_context(tc.psum_pool(name="aps", bufs=4))

        xs_v = x_scale.rearrange("(m p) j -> p m j", p=P)
        xs0 = keep.tile([P, 4, 16], F32, name="xs0")
        nc.scalar.dma_start(out=xs0[:], in_=xs_v[:, 0:4, :])
        ws = keep.tile([P, 16], F32, name="ws")
        for a in range(4):
            nc.scalar.dma_start(out=ws[32 * a : 32 * a + 32, :], in_=w_scale[a].partition_broadcast(32))
        bb = keep.tile([P, 4], BF16, name="bb")
        nc.scalar.dma_start(out=bb[:], in_=b.rearrange("(p a) -> p a", a=4))
        xs1 = keep.tile([P, 12, 16], F32, name="xs1")

        w_v = w_bytes.rearrange("(p a) k -> p a k", a=4)
        x_v = x_bytes.rearrange("(m p) k -> p m k", p=P)
        xb = {}
        for h, g in ((0, 0), (1, 0), (1, 3), (0, 3)):
            t = byts.tile([P, 2, KP], U8, name="bhalf")
            nc.sync.dma_start(out=t[:], in_=x_v[:, 2 * h : 2 * h + 2, KP * g : KP * g + KP])
            xb[0, 2 * h, g] = (t, 0, 0)
            xb[0, 2 * h + 1, g] = (t, 1, 0)
        for g in (1, 2):
            t = byts.tile([P, 4, KP], U8, name="byt")
            nc.sync.dma_start(out=t[:], in_=x_v[:, 0:4, KP * g : KP * g + KP])
            for m in range(4):
                xb[0, m, g] = (t, m, 0)
        for v, j, gs in ((w_v, 1, (0, 3, 1, 2)),):
            for g in gs:
                t = byts.tile([P, 4, KP], U8, name="byt")
                nc.sync.dma_start(out=t[:], in_=v[:, 0:4, KP * g : KP * g + KP])
                for m in range(4):
                    xb[j, m, g] = (t, m, 0)
        nc.sync.dma_start(out=xs1[:], in_=xs_v[:, 4:16, :])
        for M in range(1, 4):
            t = bigb.tile([P, 4, K], U8, name="big")
            nc.sync.dma_start(out=t[:], in_=x_v[:, 4 * M : 4 * M + 4, :])
            for m in range(4):
                for g in range(4):
                    if M < 3:
                        xb[M + 1, m, g] = (t, m, KP * g)
                    else:
                        xb[4 + m // 2, m % 2, g] = (t, m, KP * g)

        ident = keep.tile([P, P], F32, name="ident")
        make_identity(nc, ident[:])
        b32 = keep.tile([P, 4], F32, name="b32")
        nc.gpsimd.tensor_copy(out=b32[:], in_=bb[:])
        b02 = keep.tile([P, 4], F32, name="b02")
        nc.gpsimd.tensor_scalar(out=b02[:], in0=bb[:], scalar1=SLOPE, scalar2=None, op0=MULT)

        NT = [4, 4, 4, 4, 2, 2]
        FIRST = [0, 0, 4, 8, 12, 14]

        def src(j, g, m, q):
            t, mi, c = xb[j, m, g]
            return t[:, mi, c + 128 * q : c + 128 * q + 128]

        def scl(j, g, m, q):
            c = 4 * g + q
            if j == 1:
                return ws[:, c : c + 1]
            if j == 0:
                return xs0[:, m, c : c + 1]
            return xs1[:, FIRST[j] - 4 + m, c : c + 1]

        wide, grouped, codes, scales = {}, {}, {}, {}

        def lists(j):
            nt = NT[j]
            v = [(g, m, q) for g in range(4) for m in range(nt) for q in range(4) if g < 3 or m < nt - S3[j]]
            s = [(3, m, q) for m in reversed(range(nt - S3[j], nt)) for q in range(4)]
            return v, s

        S3 = [3,3,3,3,1,1]

        def widen_v(j, i):
            v = lists(j)[0]
            n = len(v) // 4
            for g, m, q in v[n * i : n * i + n]:
                if (j, g) not in wide:
                    wv = wid.tile([P, 4, 2, 256], BF16, name="wv", align_bytes=64)
                    wide[j, g] = wv
                s = src(j, g, m, q).bitcast(FP8)
                if g < 3:
                    o = wide[j, g][:, m, :, 64 * q : 64 * q + 64].rearrange("p u (b e) -> p b u e", e=16)
                    s = s.rearrange("p (b u e) -> p b u e", b=4, u=2)
                else:
                    o = wide[j, g][:, m, :, :].rearrange("p u e -> p (u e)")[:, 128 * q : 128 * q + 128]
                nc.vector.tensor_scalar(out=o, in0=s, scalar1=scl(j, g, m, q), scalar2=None, op0=MULT)

        def widen_3(j, i):
            v = lists(j)[1]
            n = len(v) // 4
            for g, m, q in v[n * i : n * i + n]:
                if (j, g) not in wide:
                    wv = wid.tile([P, 4, 2, 256], BF16, name="wv", align_bytes=64)
                    wide[j, g] = wv
                o = wide[j, g][:, m, :, :].rearrange("p u e -> p (u e)")[:, 128 * q : 128 * q + 128]
                s = src(j, g, m, q).bitcast(FP8)
                nc.scalar.activation(out=o, in_=s, func=ACT.Copy, scale=scl(j, g, m, q))

        def together(j, g):
            if j == 5 and g >= 2:
                return [g]
            return [g - g % 2, g - g % 2 + 1]

        def turn(j, g):
            nt = NT[j]
            ps = together(j, g)
            if g == ps[0]:
                gt = grp.tile([P, 8, P, 4], BF16, name="gt", align_bytes=64)
                for x in ps:
                    grouped[j, x] = gt
            c = nt * (g - ps[0])
            for h in range(nt // 2):
                xt = tps.tile([P, 2, 2, P], F32, name="xt")
                for mm in range(2):
                    m = 2 * h + mm
                    for u in range(2):
                        if g < 3:
                            w_in = wide[j, g][:, m, u, :].bitcast(F32)
                        else:
                            w_in = wide[j, g][:, m, :, :].rearrange("p u e -> p (u e)").bitcast(F32)[:, u : 256 : 2]
                        nc.tensor.transpose(xt[:, mm, u, :], w_in, ident[:])
                nc.scalar.copy(
                    out=grouped[j, g][:, c + 2 * h : c + 2 * h + 2, :, :].bitcast(F32),
                    in_=xt[:].rearrange("p m u r -> p m r u"),
                )

        def quant(j, g):
            ps = together(j, g)
            if g != ps[-1]:
                return
            nt = NT[j]
            w = nt * P * len(ps)
            pool = wcp if j == 1 else xcp
            cd = pool.tile([P, 1024], U32, name="cd", align_bytes=64)
            sc = pool.tile([P, 1024], U8, name="sc", align_bytes=64)
            for x in ps:
                o = nt * P * (x - ps[0])
                codes[j, x], scales[j, x] = cd[:, o : o + nt * P], sc[:, o : o + nt * P]
            nc.vector.quantize_mx(
                out=cd[:, 0:w].bitcast(FP8X4),
                scales=sc[:, 0:w],
                in_=grouped[j, g][:, 0 : nt * len(ps), :, :].rearrange("p m r t -> p (m r t)"),
            )

        accs, lows = {}, {}

        def mm(j, n, g):
            w = NT[j] * P
            if g == 0:
                acc = aps.tile([P, 512], F32, name="acc")
                accs[j, n] = acc
            nc.tensor.matmul_mx(
                out=accs[j, n][:, 0:w],
                lhsT=codes[1, g][:, 128 * n : 128 * n + 128].bitcast(FP8X4),
                lhsT_scale=scales[1, g][:, 128 * n : 128 * n + 128],
                rhs=codes[j, g].bitcast(FP8X4),
                rhs_scale=scales[j, g],
                start=(g == 0),
                stop=(g == 3),
            )

        def epi_s(j, n):
            w = NT[j] * P
            low = ypool.tile([P, 512], F32, name="low")
            lows[j, n] = low
            nc.scalar.activation(
                out=low[:, 0:w], in_=accs[j, n][:, 0:w], func=ACT.Identity, bias=b02[:, n : n + 1], scale=SLOPE
            )

        def epi_v(j, n):
            w = NT[j] * P
            y = ypool.tile([P, 512], F32, name="y")
            nc.vector.scalar_tensor_tensor(
                out=y[:, 0:w], in0=accs[j, n][:, 0:w], scalar=b32[:, n : n + 1], in1=lows[j, n][:, 0:w], op0=ADD, op1=MAX
            )
            i0 = FIRST[j] // 2
            nc.sync.dma_start(
                out=out_v[n, :, i0 : i0 + NT[j] // 2, :], in_=y[:, 0:w].rearrange("p (i t) -> p i t", t=256)
            )

        mms, epis = {}, {}
        for j, s0 in ((0, 11), (2, 15), (3, 19)):
            for n in range(4):
                mms[s0 + n] = [(j, n, g) for g in range(4)]
                epis[s0 + n + 1] = [(j, n)]
        mms[23] = [(4, n, g) for n in (0, 1) for g in range(4)]

        pinned = ctx.enter_context(
            tc.manual_schedule(
                engines={mybir.EngineType.PE, mybir.EngineType.Activation, mybir.EngineType.DVE, mybir.EngineType.SP}
            )
        )
        for s in range(24):
            j, i = divmod(s, 4)
            widen_3(j, i)
            for e in epis.get(s, []):
                epi_s(*e)
            if s >= 2:
                turn((s - 2) // 4, (s - 2) % 4)
            for x in mms.get(s, []):
                mm(*x)
            widen_v(j, i)
            if s >= 3:
                quant((s - 3) // 4, (s - 3) % 4)
            for e in epis.get(s, []):
                epi_v(*e)
        epi_s(4, 0)
        epi_v(4, 0)
        quant(5, 1)
        turn(5, 2)
        turn(5, 3)
        epi_s(4, 1)
        for n in (2, 3):
            for g in range(4):
                mm(4, n, g)
        quant(5, 2)
        epi_v(4, 1)
        for n in (0, 1):
            for g in range(3):
                mm(5, n, g)
        quant(5, 3)
        for n in (2, 3):
            epi_s(4, n)
            epi_v(4, n)
        for n in (0, 1):
            mm(5, n, 3)
        for n in (2, 3):
            for g in range(4):
                mm(5, n, g)
        for n in range(4):
            epi_s(5, n)
            epi_v(5, n)
